import numpy as np
import ml_dtypes


def mxq(x, axis, fmt="e4m3"):
    dtype, down = {"e4m3": (ml_dtypes.float8_e4m3fn, 7), "e5m2": (ml_dtypes.float8_e5m2, 14)}[fmt]
    v = np.moveaxis(np.asarray(x, np.float32).astype(ml_dtypes.bfloat16).astype(np.float64), axis, -1)
    blocks = v.reshape(v.shape[:-1] + (-1, 32))
    amax = np.abs(blocks).max(-1, keepdims=True)
    byte = np.maximum(np.where(amax > 0, np.frexp(amax)[1] - 1 + 127, 0) - down, 1)
    scale = np.exp2(byte - 127.0)
    codes = (blocks / scale).astype(np.float32).astype(dtype).astype(np.float64)
    return np.moveaxis((codes * scale).reshape(v.shape), -1, axis)


WIDE = False


def mx_kscale(k, group=512):
    if not WIDE:
        return np.ones(k)
    levels = np.array([10, -10, 5, -5, 0])
    if group != 512:
        return np.exp2(np.random.permutation(np.resize(levels, k // group))).repeat(group)
    if k % 512:
        return np.exp2(np.random.permutation(np.resize(levels, k // 32))).repeat(32)
    a = np.empty((k // 512, 16))
    for p in range(k // 512):
        a[p, :8] = np.random.permutation(np.resize(levels, 8))
        for g in range(8):
            far = levels[np.abs(levels - a[p, g]) >= 10]
            a[p, g + 8] = far[np.random.randint(len(far))]
    return np.exp2(a.ravel()).repeat(32)


def f64(x):
    return np.asarray(x).astype(np.float64)


G, D, M, O, N = 2, 256, 128, 256, 512


def setup_inputs():
    n = np.random.standard_normal
    s_d = mx_kscale(D, 0)
    s_o = mx_kscale(O, 0)
    return {
        "x": (n((G, D, N)) * s_d[:, None]).astype(np.float32),
        "w1": (n((G, D, M)) / np.sqrt(D) / s_d[:, None]).astype(np.float32),
        "w2": (n((G, D, M)) / np.sqrt(D) / s_d[:, None]).astype(np.float32),
        "tp": (np.random.uniform(0.6, 2.0, (G, M, 1))).astype(np.float32),
        "wo": (n((G, O, M)) / np.sqrt(O) / s_o[:, None]).astype(np.float32),
        "dy": (n((G, O, N)) * s_o[:, None]).astype(np.float32),
        "og": (np.random.uniform(0.3, 1.0, (G, M, 1))).astype(np.float32),
        "base": (0.2 * n((G, M, N))).astype(np.float32),
    }


def reference(x, w1, w2, tp, wo, dy, og, base):
    w1q = mxq(f64(w1), 1, "e4m3")
    xq = mxq(f64(x), 1, "e4m3")
    z1 = w1q.transpose(0, 2, 1) @ xq
    w2q = mxq(f64(w2), 1, "e4m3")
    z2 = w2q.transpose(0, 2, 1) @ xq
    se = np.exp(z1 * f64(tp)) + np.exp(z2 * f64(tp))
    woq = mxq(f64(wo), 1, "e4m3")
    dyq = mxq(f64(dy), 1, "e4m3")
    c0 = woq.transpose(0, 2, 1) @ dyq
    dse = c0 / f64(tp) / se
    dz1 = dse * np.exp(z1 * f64(tp)) * f64(tp)
    kdz1 = dz1 * 2.0
    kdse = kdz1 * f64(tp) * np.exp(z1 * f64(tp))
    kse = kdse * c0 / f64(tp) / np.square(se) * (-1.0)
    kz1 = kdz1 * f64(tp) * dse * np.exp(z1 * f64(tp)) * f64(tp) + kse * np.exp(z1 * f64(tp)) * f64(tp)
    y = kz1 * f64(og) + f64(base)
    return y

@@ -1,0 +1,227 @@
+from contextlib import ExitStack
+
+import concourse.mybir as mybir
+
+G, D, M, N = 2, 256, 128, 512
+FLOPS = 3 * 2 * G * D * M * N
+
+F32 = mybir.dt.float32
+BF16 = mybir.dt.bfloat16
+U32 = mybir.dt.uint32
+U8 = mybir.dt.uint8
+FP8X4 = mybir.dt.float8_e4m3fn_x4
+ALU = mybir.AluOpType
+ACT = mybir.ActivationFunctionType
+
+P = 128
+ROWS = 64
+PACK = 4
+CH = 128
+HALF = 256
+
+
+def tile_rows_gpsoftmaxoftwo_kernel(tc, x, w1, w2, tp, wo, dy, og, base, out):
+    nc = tc.nc
+    with ExitStack() as ctx:
+        sb = ctx.enter_context(tc.tile_pool(name="sb", bufs=1))
+        ps = ctx.enter_context(tc.psum_pool(name="ps", bufs=1))
+        ctx.enter_context(tc.manual_schedule())
+
+        def load_rows(name, src, cols):
+            width = cols.stop - cols.start
+            raw = sb.tile([P, PACK, width], F32, name=name)
+            nc.sync.dma_start(out=raw[:], in_=src.rearrange("g (p j) n -> (g p) j n", j=PACK)[:, :, cols])
+            return raw
+
+        def interleave(name, raw, first, on_scalar):
+            words = sb.tile([P, CH, PACK], BF16, name=name, align_bytes=64)
+            src = raw[:, :, first : first + CH].rearrange("p j (c i) -> p c j i", i=4)
+            dst = words[:].rearrange("p (c i) j -> p c j i", i=4)
+            if on_scalar:
+                nc.scalar.activation(out=dst, in_=src, func=ACT.Copy)
+            else:
+                nc.vector.tensor_copy(out=dst, in_=src)
+            return words
+
+        def quantise(name, words):
+            codes = sb.tile([P, CH], U32, name=name + "_codes", align_bytes=64)
+            scales = sb.tile([P, CH], U8, name=name + "_scales", align_bytes=64)
+            nc.vector.quantize_mx(
+                out=codes[:].bitcast(FP8X4), scales=scales[:], in_=words[:].rearrange("p c j -> p (c j)")
+            )
+            return codes, scales
+
+        def product(dst, g, weights, moving):
+            rows = slice(ROWS * g, ROWS * (g + 1))
+            nc.tensor.matmul_mx(
+                out=dst,
+                lhsT=weights[0][rows, :].bitcast(FP8X4),
+                lhsT_scale=weights[1][rows, :],
+                rhs=moving[0][rows, :].bitcast(FP8X4),
+                rhs_scale=moving[1][rows, :],
+                start=True,
+                stop=True,
+            )
+
+        halves = [slice(HALF * h, HALF * (h + 1)) for h in range(2)]
+        all_m = slice(0, M)
+
+        rows4 = sb.tile([P, 128], F32, name="rows4", align_bytes=64)
+        nc.vector.memset(rows4[:], 0.0)
+        x_raw = {}
+        dy_raw = {}
+        x_raw[0] = load_rows("x_raw0", x, halves[0])
+        for s, vec in enumerate((tp, og)):
+            nc.sync.dma_start(
+                out=rows4[0:P:32, 64 * s : 64 * (s + 1)].rearrange("q (g i) -> q g i", g=G),
+                in_=vec.rearrange("g (q i) o -> q g (i o)", q=4),
+            )
+        w2_raw = load_rows("w2_raw", w2, all_m)
+        w1_raw = load_rows("w1_raw", w1, all_m)
+        wo_raw = load_rows("wo_raw", wo, all_m)
+        dy_raw[0] = load_rows("dy_raw0", dy, halves[0])
+        x_raw[1] = load_rows("x_raw1", x, halves[1])
+        dy_raw[1] = load_rows("dy_raw1", dy, halves[1])
+        base_sb = []
+        for g in range(G):
+            b = sb.tile([P, N], F32, name="base%d" % g)
+            nc.sync.dma_start(out=b[:], in_=base[g])
+            base_sb.append(b)
+
+        cols4 = sb.tile([P, 128], F32, name="cols4", align_bytes=64)
+        half_tp = sb.tile([P, G], F32, name="half_tp")
+        gain = sb.tile([P, G], F32, name="gain")
+
+        zz = {}
+        cc = {}
+        for g in range(G):
+            for h in range(2):
+                zz[g, h] = ps.tile([P, 2, HALF], F32, name="zz%d%d" % (g, h))
+                cc[g, h] = ps.tile([P, HALF], F32, name="cc%d%d" % (g, h))
+
+        xw = {}
+        xq = {}
+        dw = {}
+        dq = {}
+        t = {}
+
+        def cp_x(c, on_scalar):
+            xw[c] = interleave("xw%d" % c, x_raw[c // 2], CH * (c % 2), on_scalar)
+
+        def cp_dy(c, on_scalar):
+            dw[c] = interleave("dw%d" % c, dy_raw[c // 2], CH * (c % 2), on_scalar)
+
+        def q_x(c):
+            xq[c] = quantise("xq%d" % c, xw[c])
+
+        def q_dy(c):
+            dq[c] = quantise("dq%d" % c, dw[c])
+
+        def mm_z(which, wq, h):
+            for g in range(G):
+                for c in range(2):
+                    product(zz[g, h][:, which, CH * c : CH * (c + 1)], g, wq, xq[2 * h + c])
+
+        def mm_c(wq, h):
+            for g in range(G):
+                for c in range(2):
+                    product(cc[g, h][:, CH * c : CH * (c + 1)], g, wq, dq[2 * h + c])
+
+        def new(name, g, h):
+            t[name, g, h] = sb.tile([P, HALF], F32, name="%s%d%d" % (name, g, h))
+            return t[name, g, h][:]
+
+        def a1(g, h):
+            nc.scalar.copy(out=new("z2", g, h), in_=zz[g, h][:, 1, :])
+
+        def v1(g, h):
+            nc.vector.tensor_tensor(out=new("d", g, h), in0=zz[g, h][:, 0, :], in1=t["z2", g, h][:], op=ALU.subtract)
+
+        def a2(g, h):
+            nc.scalar.activation(out=new("th", g, h), in_=t["d", g, h][:], func=ACT.Tanh, scale=half_tp[:, g : g + 1])
+
+        def v2(g, h):
+            nc.vector.scalar_tensor_tensor(
+                out=new("m", g, h), in0=t["th", g, h][:], scalar=1.0, in1=cc[g, h][:], op0=ALU.add, op1=ALU.mult
+            )
+
+        def a3(g, h):
+            nc.scalar.activation(out=new("s", g, h), in_=t["m", g, h][:], func=ACT.Square)
+
+        def v3(g, h):
+            nc.vector.scalar_tensor_tensor(
+                out=new("r", g, h), in0=t["th", g, h][:], scalar=1.0, in1=t["s", g, h][:], op0=ALU.subtract, op1=ALU.mult
+            )
+
+        def v4(g, h):
+            nc.vector.scalar_tensor_tensor(
+                out=new("y", g, h),
+                in0=t["r", g, h][:],
+                scalar=gain[:, g : g + 1],
+                in1=base_sb[g][:, halves[h]],
+                op0=ALU.mult,
+                op1=ALU.add,
+            )
+            nc.sync.dma_start(out=out[g, :, halves[h]], in_=t["y", g, h][:])
+
+        cp_x(0, False)
+        cp_x(1, True)
+        q_x(0)
+        w2w = interleave("w2w", w2_raw, 0, False)
+        q_x(1)
+        w2q = quantise("w2q", w2w)
+        mm_z(1, w2q, 0)
+        nc.vector.transpose(out=cols4[:], in_=rows4[:])
+        w1w = interleave("w1w", w1_raw, 0, False)
+        a1(0, 0)
+        a1(1, 0)
+        w1q = quantise("w1q", w1w)
+        mm_z(0, w1q, 0)
+        nc.vector.tensor_scalar(out=half_tp[:], in0=cols4[:, 0:64:32], scalar1=0.5, scalar2=None, op0=ALU.mult)
+        nc.vector.scalar_tensor_tensor(
+            out=gain[:], in0=cols4[:, 0:64:32], scalar=-0.25, in1=cols4[:, 64:128:32], op0=ALU.mult, op1=ALU.mult
+        )
+        wow = interleave("wow", wo_raw, 0, False)
+        v1(0, 0)
+        woq = quantise("woq", wow)
+        v1(1, 0)
+        a2(0, 0)
+        a2(1, 0)
+        cp_dy(0, False)
+        cp_dy(1, True)
+        q_dy(0)
+        q_dy(1)
+        mm_c(woq, 0)
+        cp_x(3, True)
+        cp_x(2, False)
+        v2(0, 0)
+        q_x(2)
+        v2(1, 0)
+        q_x(3)
+        mm_z(1, w2q, 1)
+        mm_z(0, w1q, 1)
+        a3(0, 0)
+        a3(1, 0)
+        cp_dy(3, True)
+        cp_dy(2, False)
+        v3(0, 0)
+        q_dy(2)
+        a1(0, 1)
+        a1(1, 1)
+        q_dy(3)
+        mm_c(woq, 1)
+        v1(0, 1)
+        v1(1, 1)
+        a2(0, 1)
+        a2(1, 1)
+        v3(1, 0)
+        v4(0, 0)
+        v2(0, 1)
+        v2(1, 1)
+        a3(0, 1)
+        a3(1, 1)
+        v4(1, 0)
+        v3(0, 1)
+        v3(1, 1)
+        v4(0, 1)
+        v4(1, 1)

@@ -92,11 +92,13 @@ def tile_rows_gpsoftmaxoftwo_kernel(tc, x, w1, w2, tp, wo, dy, og, base, out):
         half_tp = sb.tile([P, G], F32, name="half_tp")
         gain = sb.tile([P, G], F32, name="gain")
 
-        zz = {}
+        z1 = {}
+        z2 = {}
         cc = {}
         for g in range(G):
+            z1[g] = ps.tile([P, N], F32, name="z1_%d" % g)
+            z2[g] = ps.tile([P, N], F32, name="z2_%d" % g)
             for h in range(2):
-                zz[g, h] = ps.tile([P, 2, HALF], F32, name="zz%d%d" % (g, h))
                 cc[g, h] = ps.tile([P, HALF], F32, name="cc%d%d" % (g, h))
 
         xw = {}
@@ -117,25 +119,27 @@ def tile_rows_gpsoftmaxoftwo_kernel(tc, x, w1, w2, tp, wo, dy, og, base, out):
         def q_dy(c):
             dq[c] = quantise("dq%d" % c, dw[c])
 
-        def mm_z(which, wq, h):
-            for g in range(G):
-                for c in range(2):
-                    product(zz[g, h][:, which, CH * c : CH * (c + 1)], g, wq, xq[2 * h + c])
+        def mm_z(z, wq, g, c):
+            product(z[g][:, CH * c : CH * (c + 1)], g, wq, xq[c])
 
-        def mm_c(wq, h):
+        def mm_c(c):
             for g in range(G):
-                for c in range(2):
-                    product(cc[g, h][:, CH * c : CH * (c + 1)], g, wq, dq[2 * h + c])
+                product(cc[g, c // 2][:, CH * (c % 2) : CH * (c % 2 + 1)], g, woq, dq[c])
+
+        def mm_zz(c):
+            for z, wq in ((z2, w2q), (z1, w1q)):
+                for g in range(G):
+                    mm_z(z, wq, g, c)
 
         def new(name, g, h):
             t[name, g, h] = sb.tile([P, HALF], F32, name="%s%d%d" % (name, g, h))
             return t[name, g, h][:]
 
         def a1(g, h):
-            nc.scalar.copy(out=new("z2", g, h), in_=zz[g, h][:, 1, :])
+            nc.scalar.copy(out=new("z2", g, h), in_=z2[g][:, halves[h]])
 
         def v1(g, h):
-            nc.vector.tensor_tensor(out=new("d", g, h), in0=zz[g, h][:, 0, :], in1=t["z2", g, h][:], op=ALU.subtract)
+            nc.vector.tensor_tensor(out=new("d", g, h), in0=z1[g][:, halves[h]], in1=t["z2", g, h][:], op=ALU.subtract)
 
         def a2(g, h):
             nc.scalar.activation(out=new("th", g, h), in_=t["d", g, h][:], func=ACT.Tanh, scale=half_tp[:, g : g + 1])
@@ -166,50 +170,56 @@ def tile_rows_gpsoftmaxoftwo_kernel(tc, x, w1, w2, tp, wo, dy, og, base, out):
 
         cp_x(0, False)
         cp_x(1, True)
-        q_x(0)
         w2w = interleave("w2w", w2_raw, 0, False)
+        q_x(0)
         q_x(1)
         w2q = quantise("w2q", w2w)
-        mm_z(1, w2q, 0)
+        for g in range(G):
+            for c in range(2):
+                mm_z(z2, w2q, g, c)
+        w1w = interleave("w1w", w1_raw, 0, True)
         nc.vector.transpose(out=cols4[:], in_=rows4[:])
-        w1w = interleave("w1w", w1_raw, 0, False)
-        a1(0, 0)
-        a1(1, 0)
         w1q = quantise("w1q", w1w)
-        mm_z(0, w1q, 0)
+        for g in range(G):
+            for c in range(2):
+                mm_z(z1, w1q, g, c)
+        wow = interleave("wow", wo_raw, 0, False)
         nc.vector.tensor_scalar(out=half_tp[:], in0=cols4[:, 0:64:32], scalar1=0.5, scalar2=None, op0=ALU.mult)
         nc.vector.scalar_tensor_tensor(
             out=gain[:], in0=cols4[:, 0:64:32], scalar=-0.25, in1=cols4[:, 64:128:32], op0=ALU.mult, op1=ALU.mult
         )
-        wow = interleave("wow", wo_raw, 0, False)
-        v1(0, 0)
+        a1(0, 0)
+        a1(1, 0)
         woq = quantise("woq", wow)
-        v1(1, 0)
-        a2(0, 0)
-        a2(1, 0)
         cp_dy(0, False)
         cp_dy(1, True)
+        v1(0, 0)
         q_dy(0)
+        mm_c(0)
+        v1(1, 0)
         q_dy(1)
-        mm_c(woq, 0)
-        cp_x(3, True)
+        mm_c(1)
         cp_x(2, False)
-        v2(0, 0)
+        a2(0, 0)
+        cp_x(3, True)
         q_x(2)
-        v2(1, 0)
+        mm_zz(2)
+        a2(1, 0)
+        v2(0, 0)
         q_x(3)
-        mm_z(1, w2q, 1)
-        mm_z(0, w1q, 1)
-        a3(0, 0)
-        a3(1, 0)
-        cp_dy(3, True)
+        mm_zz(3)
+        v2(1, 0)
         cp_dy(2, False)
-        v3(0, 0)
+        a3(0, 0)
+        cp_dy(3, True)
         q_dy(2)
+        mm_c(2)
+        v3(0, 0)
         a1(0, 1)
         a1(1, 1)
+        a3(1, 0)
         q_dy(3)
-        mm_c(woq, 1)
+        mm_c(3)
         v1(0, 1)
         v1(1, 1)
         a2(0, 1)

@@ -33,9 +33,9 @@ def tile_rows_gpsoftmaxoftwo_kernel(tc, x, w1, w2, tp, wo, dy, og, base, out):
             nc.sync.dma_start(out=raw[:], in_=src.rearrange("g (p j) n -> (g p) j n", j=PACK)[:, :, cols])
             return raw
 
-        def interleave(name, raw, first, on_scalar):
-            words = sb.tile([P, CH, PACK], BF16, name=name, align_bytes=64)
-            src = raw[:, :, first : first + CH].rearrange("p j (c i) -> p c j i", i=4)
+        def interleave(name, raw, first, on_scalar, width=CH):
+            words = sb.tile([P, width, PACK], BF16, name=name, align_bytes=64)
+            src = raw[:, :, first : first + width].rearrange("p j (c i) -> p c j i", i=4)
             dst = words[:].rearrange("p (c i) j -> p c j i", i=4)
             if on_scalar:
                 nc.scalar.activation(out=dst, in_=src, func=ACT.Copy)
@@ -44,8 +44,9 @@ def tile_rows_gpsoftmaxoftwo_kernel(tc, x, w1, w2, tp, wo, dy, og, base, out):
             return words
 
         def quantise(name, words):
-            codes = sb.tile([P, CH], U32, name=name + "_codes", align_bytes=64)
-            scales = sb.tile([P, CH], U8, name=name + "_scales", align_bytes=64)
+            width = words.shape[1]
+            codes = sb.tile([P, width], U32, name=name + "_codes", align_bytes=64)
+            scales = sb.tile([P, width], U8, name=name + "_scales", align_bytes=64)
             nc.vector.quantize_mx(
                 out=codes[:].bitcast(FP8X4), scales=scales[:], in_=words[:].rearrange("p c j -> p (c j)")
             )
@@ -78,9 +79,9 @@ def tile_rows_gpsoftmaxoftwo_kernel(tc, x, w1, w2, tp, wo, dy, og, base, out):
             )
         w2_raw = load_rows("w2_raw", w2, all_m)
         w1_raw = load_rows("w1_raw", w1, all_m)
+        x_raw[1] = load_rows("x_raw1", x, halves[1])
         wo_raw = load_rows("wo_raw", wo, all_m)
         dy_raw[0] = load_rows("dy_raw0", dy, halves[0])
-        x_raw[1] = load_rows("x_raw1", x, halves[1])
         dy_raw[1] = load_rows("dy_raw1", dy, halves[1])
         base_sb = []
         for g in range(G):
@@ -118,6 +119,16 @@ def tile_rows_gpsoftmaxoftwo_kernel(tc, x, w1, w2, tp, wo, dy, og, base, out):
 
         def q_dy(c):
             dq[c] = quantise("dq%d" % c, dw[c])
+
+        def q_half(name, words, table, h):
+            codes, scales = quantise(name, words)
+            for c in range(2):
+                table[2 * h + c] = (codes[:, CH * c : CH * (c + 1)], scales[:, CH * c : CH * (c + 1)])
+
+        def mm_c_half(h):
+            for g in range(G):
+                for c in range(2):
+                    product(cc[g, h][:, CH * c : CH * (c + 1)], g, woq, dq[2 * h + c])
 
         def mm_z(z, wq, g, c):
             product(z[g][:, CH * c : CH * (c + 1)], g, wq, xq[c])
@@ -157,6 +168,20 @@ def tile_rows_gpsoftmaxoftwo_kernel(tc, x, w1, w2, tp, wo, dy, og, base, out):
                 out=new("r", g, h), in0=t["th", g, h][:], scalar=1.0, in1=t["s", g, h][:], op0=ALU.subtract, op1=ALU.mult
             )
 
+        def ah(g, h):
+            nc.scalar.activation(out=new("q", g, h), in_=t["th", g, h][:], func=ACT.Square, bias=1.0)
+
+        def vh(g, h):
+            nc.vector.scalar_tensor_tensor(
+                out=new("f", g, h), in0=t["th", g, h][:], scalar=1.0, in1=t["q", g, h][:], op0=ALU.subtract, op1=ALU.mult
+            )
+
+        def asq(g, h):
+            nc.scalar.activation(out=new("s", g, h), in_=cc[g, h][:], func=ACT.Square)
+
+        def vr(g, h):
+            nc.vector.tensor_tensor(out=new("r", g, h), in0=t["s", g, h][:], in1=t["f", g, h][:], op=ALU.mult)
+
         def v4(g, h):
             nc.vector.scalar_tensor_tensor(
                 out=new("y", g, h),
@@ -183,55 +208,36 @@ def tile_rows_gpsoftmaxoftwo_kernel(tc, x, w1, w2, tp, wo, dy, og, base, out):
         for g in range(G):
             for c in range(2):
                 mm_z(z1, w1q, g, c)
-        wow = interleave("wow", wo_raw, 0, False)
         nc.vector.tensor_scalar(out=half_tp[:], in0=cols4[:, 0:64:32], scalar1=0.5, scalar2=None, op0=ALU.mult)
         nc.vector.scalar_tensor_tensor(
             out=gain[:], in0=cols4[:, 0:64:32], scalar=-0.25, in1=cols4[:, 64:128:32], op0=ALU.mult, op1=ALU.mult
         )
+        x1w = interleave("x1w", x_raw[1], 0, False, HALF)
         a1(0, 0)
         a1(1, 0)
-        woq = quantise("woq", wow)
-        cp_dy(0, False)
-        cp_dy(1, True)
         v1(0, 0)
-        q_dy(0)
-        mm_c(0)
+        q_half("x1q", x1w, xq, 1)
         v1(1, 0)
-        q_dy(1)
-        mm_c(1)
-        cp_x(2, False)
+        for z, wq in ((z2, w2q), (z1, w1q)):
+            for g in range(G):
+                for c in (2, 3):
+                    mm_z(z, wq, g, c)
+        wow = interleave("wow", wo_raw, 0, True)
+        d0w = interleave("d0w", dy_raw[0], 0, False, HALF)
+        woq = quantise("woq", wow)
         a2(0, 0)
-        cp_x(3, True)
-        q_x(2)
-        mm_zz(2)
         a2(1, 0)
-        v2(0, 0)
-        q_x(3)
-        mm_zz(3)
-        v2(1, 0)
-        cp_dy(2, False)
-        a3(0, 0)
-        cp_dy(3, True)
-        q_dy(2)
-        mm_c(2)
-        v3(0, 0)
+        q_half("d0q", d0w, dq, 0)
+        mm_c_half(0)
         a1(0, 1)
         a1(1, 1)
-        a3(1, 0)
-        q_dy(3)
-        mm_c(3)
         v1(0, 1)
         v1(1, 1)
-        a2(0, 1)
-        a2(1, 1)
-        v3(1, 0)
-        v4(0, 0)
-        v2(0, 1)
-        v2(1, 1)
-        a3(0, 1)
-        a3(1, 1)
-        v4(1, 0)
-        v3(0, 1)
-        v3(1, 1)
-        v4(0, 1)
-        v4(1, 1)
+        d1w = interleave("d1w", dy_raw[1], 0, True, HALF)
+        v2(0, 0)
+        v2(1, 0)
+        q_half("d1q", d1w, dq, 1)
+        mm_c_half(1)
+        for step, h in ((a3, 0), (a2, 1), (ah, 1), (v3, 0), (v4, 0), (vh, 1), (asq, 1), (vr, 1), (v4, 1)):
+            for g in range(G):
+                step(g, h)

from contextlib import ExitStack

import concourse.mybir as mybir

G, D, M, N = 2, 256, 128, 512
FLOPS = 3 * 2 * G * D * M * N

F32 = mybir.dt.float32
BF16 = mybir.dt.bfloat16
U32 = mybir.dt.uint32
U8 = mybir.dt.uint8
FP8X4 = mybir.dt.float8_e4m3fn_x4
ALU = mybir.AluOpType
ACT = mybir.ActivationFunctionType

P = 128
ROWS = 64
PACK = 4
CH = 128
HALF = 256


def tile_rows_gpsoftmaxoftwo_kernel(tc, x, w1, w2, tp, wo, dy, og, base, out):
    nc = tc.nc
    with ExitStack() as ctx:
        sb = ctx.enter_context(tc.tile_pool(name="sb", bufs=1))
        ps = ctx.enter_context(tc.psum_pool(name="ps", bufs=1))
        ctx.enter_context(tc.manual_schedule())

        def load_rows(name, src, cols):
            width = cols.stop - cols.start
            raw = sb.tile([P, PACK, width], F32, name=name)
            nc.sync.dma_start(out=raw[:], in_=src.rearrange("g (p j) n -> (g p) j n", j=PACK)[:, :, cols])
            return raw

        def interleave(name, raw, first, on_scalar, width=CH):
            words = sb.tile([P, width, PACK], BF16, name=name, align_bytes=64)
            src = raw[:, :, first : first + width].rearrange("p j (c i) -> p c j i", i=4)
            dst = words[:].rearrange("p (c i) j -> p c j i", i=4)
            if on_scalar:
                nc.scalar.activation(out=dst, in_=src, func=ACT.Copy)
            else:
                nc.vector.tensor_copy(out=dst, in_=src)
            return words

        def quantise(name, words):
            width = words.shape[1]
            codes = sb.tile([P, width], U32, name=name + "_codes", align_bytes=64)
            scales = sb.tile([P, width], U8, name=name + "_scales", align_bytes=64)
            nc.vector.quantize_mx(
                out=codes[:].bitcast(FP8X4), scales=scales[:], in_=words[:].rearrange("p c j -> p (c j)")
            )
            return codes, scales

        def product(dst, g, weights, moving):
            rows = slice(ROWS * g, ROWS * (g + 1))
            nc.tensor.matmul_mx(
                out=dst,
                lhsT=weights[0][rows, :].bitcast(FP8X4),
                lhsT_scale=weights[1][rows, :],
                rhs=moving[0][rows, :].bitcast(FP8X4),
                rhs_scale=moving[1][rows, :],
                start=True,
                stop=True,
            )

        halves = [slice(HALF * h, HALF * (h + 1)) for h in range(2)]
        all_m = slice(0, M)

        rows4 = sb.tile([P, 128], F32, name="rows4", align_bytes=64)
        nc.vector.memset(rows4[:], 0.0)
        x_raw = {}
        dy_raw = {}
        x_raw[0] = load_rows("x_raw0", x, halves[0])
        for s, vec in enumerate((tp, og)):
            nc.sync.dma_start(
                out=rows4[0:P:32, 64 * s : 64 * (s + 1)].rearrange("q (g i) -> q g i", g=G),
                in_=vec.rearrange("g (q i) o -> q g (i o)", q=4),
            )
        w2_raw = load_rows("w2_raw", w2, all_m)
        w1_raw = load_rows("w1_raw", w1, all_m)
        x_raw[1] = load_rows("x_raw1", x, halves[1])
        wo_raw = load_rows("wo_raw", wo, all_m)
        dy_raw[0] = load_rows("dy_raw0", dy, halves[0])
        dy_raw[1] = load_rows("dy_raw1", dy, halves[1])
        base_sb = []
        for g in range(G):
            b = sb.tile([P, N], F32, name="base%d" % g)
            nc.sync.dma_start(out=b[:], in_=base[g])
            base_sb.append(b)

        cols4 = sb.tile([P, 128], F32, name="cols4", align_bytes=64)
        half_tp = sb.tile([P, G], F32, name="half_tp")
        gain = sb.tile([P, G], F32, name="gain")

        z1 = {}
        z2 = {}
        cc = {}
        for g in range(G):
            z1[g] = ps.tile([P, N], F32, name="z1_%d" % g)
            z2[g] = ps.tile([P, N], F32, name="z2_%d" % g)
            for h in range(2):
                cc[g, h] = ps.tile([P, HALF], F32, name="cc%d%d" % (g, h))

        xw = {}
        xq = {}
        dw = {}
        dq = {}
        t = {}

        def cp_x(c, on_scalar):
            xw[c] = interleave("xw%d" % c, x_raw[c // 2], CH * (c % 2), on_scalar)

        def cp_dy(c, on_scalar):
            dw[c] = interleave("dw%d" % c, dy_raw[c // 2], CH * (c % 2), on_scalar)

        def q_x(c):
            xq[c] = quantise("xq%d" % c, xw[c])

        def q_dy(c):
            dq[c] = quantise("dq%d" % c, dw[c])

        def q_half(name, words, table, h):
            codes, scales = quantise(name, words)
            for c in range(2):
                table[2 * h + c] = (codes[:, CH * c : CH * (c + 1)], scales[:, CH * c : CH * (c + 1)])

        def mm_c_half(h):
            for g in range(G):
                for c in range(2):
                    product(cc[g, h][:, CH * c : CH * (c + 1)], g, woq, dq[2 * h + c])

        def mm_z(z, wq, g, c):
            product(z[g][:, CH * c : CH * (c + 1)], g, wq, xq[c])

        def mm_c(c):
            for g in range(G):
                product(cc[g, c // 2][:, CH * (c % 2) : CH * (c % 2 + 1)], g, woq, dq[c])

        def mm_zz(c):
            for z, wq in ((z2, w2q), (z1, w1q)):
                for g in range(G):
                    mm_z(z, wq, g, c)

        def new(name, g, h):
            t[name, g, h] = sb.tile([P, HALF], F32, name="%s%d%d" % (name, g, h))
            return t[name, g, h][:]

        def a1(g, h):
            nc.scalar.copy(out=new("z2", g, h), in_=z2[g][:, halves[h]])

        def v1(g, h):
            nc.vector.tensor_tensor(out=new("d", g, h), in0=z1[g][:, halves[h]], in1=t["z2", g, h][:], op=ALU.subtract)

        def a2(g, h):
            nc.scalar.activation(out=new("th", g, h), in_=t["d", g, h][:], func=ACT.Tanh, scale=half_tp[:, g : g + 1])

        def v2(g, h):
            nc.vector.scalar_tensor_tensor(
                out=new("m", g, h), in0=t["th", g, h][:], scalar=1.0, in1=cc[g, h][:], op0=ALU.add, op1=ALU.mult
            )

        def a3(g, h):
            nc.scalar.activation(out=new("s", g, h), in_=t["m", g, h][:], func=ACT.Square)

        def v3(g, h):
            nc.vector.scalar_tensor_tensor(
                out=new("r", g, h), in0=t["th", g, h][:], scalar=1.0, in1=t["s", g, h][:], op0=ALU.subtract, op1=ALU.mult
            )

        def ah(g, h):
            nc.scalar.activation(out=new("q", g, h), in_=t["th", g, h][:], func=ACT.Square, bias=1.0)

        def vh(g, h):
            nc.vector.scalar_tensor_tensor(
                out=new("f", g, h), in0=t["th", g, h][:], scalar=1.0, in1=t["q", g, h][:], op0=ALU.subtract, op1=ALU.mult
            )

        def asq(g, h):
            nc.scalar.activation(out=new("s", g, h), in_=cc[g, h][:], func=ACT.Square)

        def vr(g, h):
            nc.vector.tensor_tensor(out=new("r", g, h), in0=t["s", g, h][:], in1=t["f", g, h][:], op=ALU.mult)

        def v4(g, h):
            nc.vector.scalar_tensor_tensor(
                out=new("y", g, h),
                in0=t["r", g, h][:],
                scalar=gain[:, g : g + 1],
                in1=base_sb[g][:, halves[h]],
                op0=ALU.mult,
                op1=ALU.add,
            )
            nc.sync.dma_start(out=out[g, :, halves[h]], in_=t["y", g, h][:])

        cp_x(0, False)
        cp_x(1, True)
        w2w = interleave("w2w", w2_raw, 0, False)
        q_x(0)
        q_x(1)
        w2q = quantise("w2q", w2w)
        for g in range(G):
            for c in range(2):
                mm_z(z2, w2q, g, c)
        w1w = interleave("w1w", w1_raw, 0, True)
        nc.vector.transpose(out=cols4[:], in_=rows4[:])
        w1q = quantise("w1q", w1w)
        for g in range(G):
            for c in range(2):
                mm_z(z1, w1q, g, c)
        nc.vector.tensor_scalar(out=half_tp[:], in0=cols4[:, 0:64:32], scalar1=0.5, scalar2=None, op0=ALU.mult)
        nc.vector.scalar_tensor_tensor(
            out=gain[:], in0=cols4[:, 0:64:32], scalar=-0.25, in1=cols4[:, 64:128:32], op0=ALU.mult, op1=ALU.mult
        )
        x1w = interleave("x1w", x_raw[1], 0, False, HALF)
        a1(0, 0)
        a1(1, 0)
        v1(0, 0)
        q_half("x1q", x1w, xq, 1)
        v1(1, 0)
        for z, wq in ((z2, w2q), (z1, w1q)):
            for g in range(G):
                for c in (2, 3):
                    mm_z(z, wq, g, c)
        wow = interleave("wow", wo_raw, 0, True)
        d0w = interleave("d0w", dy_raw[0], 0, False, HALF)
        woq = quantise("woq", wow)
        a2(0, 0)
        a2(1, 0)
        q_half("d0q", d0w, dq, 0)
        mm_c_half(0)
        a1(0, 1)
        a1(1, 1)
        v1(0, 1)
        v1(1, 1)
        d1w = interleave("d1w", dy_raw[1], 0, True, HALF)
        v2(0, 0)
        v2(1, 0)
        q_half("d1q", d1w, dq, 1)
        mm_c_half(1)
        for step, h in ((a3, 0), (a2, 1), (ah, 1), (v3, 0), (v4, 0), (vh, 1), (asq, 1), (vr, 1), (v4, 1)):
            for g in range(G):
                step(g, h)
